import numpy as np
import ml_dtypes

BF16 = ml_dtypes.bfloat16


def bf(x):
    return np.asarray(x, np.float32).astype(BF16)


def f32(x):
    return np.asarray(x, np.float32)


def f64(x):
    return np.asarray(x).astype(np.float64)


def striped(idx):
    return np.tile(idx.reshape(-1, 16).T, (8, 1))


S, K, M, N, B, Q = 512, 128, 128, 512, 2, 256


def gelu_tanh(v):
    return 0.5 * v * (1.0 + np.tanh(np.sqrt(2.0 / np.pi) * (v + 0.044715 * v**3)))


def setup_inputs():
    return {"base": bf(np.random.standard_normal((B, M, S))), "x": bf(np.random.standard_normal((K, N))), "w": bf(np.random.standard_normal((K, M)) / np.sqrt(K)), "b": f32(0.5 * np.random.standard_normal((M, 1))), "offs": striped(np.random.permutation(S))}


def reference(base, x, w, b, offs):
    idx = offs[:16].T.reshape(-1)
    z = f64(base).copy()
    for i in range(B):
        z[i][:, idx[i * Q : (i + 1) * Q]] += f64(w).T @ f64(x)[:, i * Q : (i + 1) * Q]
    return gelu_tanh(z + f64(b))

@@ -1,0 +1,55 @@
+import concourse.mybir as mybir
+from concourse.masks import make_identity
+
+BF16, F32, U16 = mybir.dt.bfloat16, mybir.dt.float32, mybir.dt.uint16
+GELU_TANH = mybir.ActivationFunctionType.Gelu_apprx_tanh
+
+P = 128
+SEQS = 2
+TOKENS = 512
+PIECE = 256
+PIECE_COLS = PIECE // 16
+
+FLOPS = 2 * P * P * SEQS * PIECE
+
+
+def tile_scatter_matmul_kernel(tc, base, x, w, b, offs, out):
+    nc = tc.nc
+    with (
+        tc.tile_pool(name="held", bufs=1) as held,
+        tc.psum_pool(name="windows", bufs=1) as windows,
+    ):
+        offsets = held.tile([P, SEQS * PIECE_COLS], U16, name="offsets")
+        nc.sync.dma_start(offsets[:], offs)
+
+        base_tiles = [held.tile([P, TOKENS], BF16, name=f"base{i}") for i in range(SEQS)]
+        x_tile = held.tile([P, SEQS * PIECE], BF16, name="x_tile")
+        w_tile = held.tile([P, P], BF16, name="w_tile")
+        bias = held.tile([P, 1], F32, name="bias")
+        nc.sync.dma_start(base_tiles[0][:], base[0])
+        nc.scalar.dma_start(base_tiles[1][:], base[1])
+        nc.sync.dma_start(x_tile[:], x)
+        nc.scalar.dma_start(w_tile[:], w)
+        nc.scalar.dma_start(bias[:], b)
+
+        identity = held.tile([P, P], BF16, name="identity")
+        make_identity(nc, identity[:])
+
+        window_tiles = [windows.tile([P, TOKENS], F32, name=f"window{i}") for i in range(SEQS)]
+        for i in range(SEQS):
+            nc.tensor.matmul(window_tiles[i][:], identity[:], base_tiles[i][:], start=True, stop=False)
+
+        for i in range(SEQS):
+            piece = offsets[:, i * PIECE_COLS : (i + 1) * PIECE_COLS]
+            nc.tensor.matmul(
+                window_tiles[i][:].indirect(piece),
+                w_tile[:],
+                x_tile[:, i * PIECE : (i + 1) * PIECE],
+                start=False,
+                stop=True,
+            )
+
+        for i in range(SEQS):
+            result = held.tile([P, TOKENS], F32, name=f"result{i}")
+            nc.scalar.activation(result[:], window_tiles[i][:], GELU_TANH, bias=bias[:])
+            nc.sync.dma_start(out[i], result[:])

@@ -19,18 +19,22 @@ def tile_scatter_matmul_kernel(tc, base, x, w, b, offs, out):
         tc.tile_pool(name="held", bufs=1) as held,
         tc.psum_pool(name="windows", bufs=1) as windows,
     ):
-        offsets = held.tile([P, SEQS * PIECE_COLS], U16, name="offsets")
-        nc.sync.dma_start(offsets[:], offs)
-
         base_tiles = [held.tile([P, TOKENS], BF16, name=f"base{i}") for i in range(SEQS)]
+        offsets = held.tile([P, SEQS * PIECE_COLS], U16, name="offsets")
         x_tile = held.tile([P, SEQS * PIECE], BF16, name="x_tile")
         w_tile = held.tile([P, P], BF16, name="w_tile")
         bias = held.tile([P, 1], F32, name="bias")
         nc.sync.dma_start(base_tiles[0][:], base[0])
         nc.scalar.dma_start(base_tiles[1][:], base[1])
-        nc.sync.dma_start(x_tile[:], x)
+        nc.sync.dma_start(offsets[:], offs)
         nc.scalar.dma_start(w_tile[:], w)
+        nc.sync.dma_start(x_tile[:], x)
         nc.scalar.dma_start(bias[:], b)
+
+        zeros = held.tile([P, 1], F32, name="zeros")
+        table_warmer = held.tile([P, 1], F32, name="table_warmer")
+        nc.vector.memset(zeros[:], 0.0)
+        nc.scalar.activation(table_warmer[:], zeros[:], GELU_TANH)
 
         identity = held.tile([P, P], BF16, name="identity")
         make_identity(nc, identity[:])

@@ -10,6 +10,8 @@ TOKENS = 512
 PIECE = 256
 PIECE_COLS = PIECE // 16
 
+WARMING_MATMULS = 3
+
 FLOPS = 2 * P * P * SEQS * PIECE
 
 
@@ -31,10 +33,15 @@ def tile_scatter_matmul_kernel(tc, base, x, w, b, offs, out):
         nc.sync.dma_start(x_tile[:], x)
         nc.scalar.dma_start(bias[:], b)
 
-        zeros = held.tile([P, 1], F32, name="zeros")
-        table_warmer = held.tile([P, 1], F32, name="table_warmer")
+        zeros = held.tile([P, TOKENS], BF16, name="zeros")
         nc.vector.memset(zeros[:], 0.0)
-        nc.scalar.activation(table_warmer[:], zeros[:], GELU_TANH)
+
+        table_warmer = held.tile([P, 1], F32, name="table_warmer")
+        nc.scalar.activation(table_warmer[:], zeros[:, 0:1], GELU_TANH)
+
+        idle_bank = windows.tile([P, TOKENS], F32, name="idle_bank")
+        for warming in range(WARMING_MATMULS):
+            nc.tensor.matmul(idle_bank[:], zeros[:, 0:P], zeros[:], start=True, stop=True)
 
         identity = held.tile([P, P], BF16, name="identity")
         make_identity(nc, identity[:])

@@ -12,11 +12,15 @@ PIECE_COLS = PIECE // 16
 
 WARMING_MATMULS = 3
 
+STORE_PIECES = 2
+
 FLOPS = 2 * P * P * SEQS * PIECE
 
 
 def tile_scatter_matmul_kernel(tc, base, x, w, b, offs, out):
     nc = tc.nc
+    run = TOKENS // STORE_PIECES
+    store_runs = [slice(r * run, (r + 1) * run) for r in range(STORE_PIECES)]
     with (
         tc.tile_pool(name="held", bufs=1) as held,
         tc.psum_pool(name="windows", bufs=1) as windows,
@@ -62,5 +66,6 @@ def tile_scatter_matmul_kernel(tc, base, x, w, b, offs, out):
 
         for i in range(SEQS):
             result = held.tile([P, TOKENS], F32, name=f"result{i}")
-            nc.scalar.activation(result[:], window_tiles[i][:], GELU_TANH, bias=bias[:])
-            nc.sync.dma_start(out[i], result[:])
+            for columns in store_runs:
+                nc.scalar.activation(result[:, columns], window_tiles[i][:, columns], GELU_TANH, bias=bias[:])
+                nc.sync.dma_start(out[i][:, columns], result[:, columns])

@@ -10,17 +10,13 @@ TOKENS = 512
 PIECE = 256
 PIECE_COLS = PIECE // 16
 
-WARMING_MATMULS = 3
-
-STORE_PIECES = 2
+WARMING_MATMULS = 2
 
 FLOPS = 2 * P * P * SEQS * PIECE
 
 
 def tile_scatter_matmul_kernel(tc, base, x, w, b, offs, out):
     nc = tc.nc
-    run = TOKENS // STORE_PIECES
-    store_runs = [slice(r * run, (r + 1) * run) for r in range(STORE_PIECES)]
     with (
         tc.tile_pool(name="held", bufs=1) as held,
         tc.psum_pool(name="windows", bufs=1) as windows,
@@ -31,10 +27,10 @@ def tile_scatter_matmul_kernel(tc, base, x, w, b, offs, out):
         w_tile = held.tile([P, P], BF16, name="w_tile")
         bias = held.tile([P, 1], F32, name="bias")
         nc.sync.dma_start(base_tiles[0][:], base[0])
-        nc.scalar.dma_start(base_tiles[1][:], base[1])
+        nc.sync.dma_start(base_tiles[1][:], base[1])
         nc.sync.dma_start(offsets[:], offs)
-        nc.scalar.dma_start(w_tile[:], w)
         nc.sync.dma_start(x_tile[:], x)
+        nc.scalar.dma_start(w_tile[:], w)
         nc.scalar.dma_start(bias[:], b)
 
         zeros = held.tile([P, TOKENS], BF16, name="zeros")
@@ -66,6 +62,5 @@ def tile_scatter_matmul_kernel(tc, base, x, w, b, offs, out):
 
         for i in range(SEQS):
             result = held.tile([P, TOKENS], F32, name=f"result{i}")
-            for columns in store_runs:
-                nc.scalar.activation(result[:, columns], window_tiles[i][:, columns], GELU_TANH, bias=bias[:])
-                nc.sync.dma_start(out[i][:, columns], result[:, columns])
+            nc.scalar.activation(result[:], window_tiles[i][:], GELU_TANH, bias=bias[:])
+            nc.sync.dma_start(out[i], result[:])

@@ -60,7 +60,8 @@ def tile_scatter_matmul_kernel(tc, base, x, w, b, offs, out):
                 stop=True,
             )
 
+        store_queues = [nc.sync, nc.scalar]
         for i in range(SEQS):
             result = held.tile([P, TOKENS], F32, name=f"result{i}")
             nc.scalar.activation(result[:], window_tiles[i][:], GELU_TANH, bias=bias[:])
-            nc.sync.dma_start(out[i], result[:])
+            store_queues[i].dma_start(out[i], result[:])

@@ -60,8 +60,7 @@ def tile_scatter_matmul_kernel(tc, base, x, w, b, offs, out):
                 stop=True,
             )
 
-        store_queues = [nc.sync, nc.scalar]
         for i in range(SEQS):
             result = held.tile([P, TOKENS], F32, name=f"result{i}")
             nc.scalar.activation(result[:], window_tiles[i][:], GELU_TANH, bias=bias[:])
-            store_queues[i].dma_start(out[i], result[:])
+            nc.scalar.dma_start(out[i], result[:])

@@ -10,6 +10,8 @@ TOKENS = 512
 PIECE = 256
 PIECE_COLS = PIECE // 16
 
+ROW_ALIGN = 256
+
 WARMING_MATMULS = 2
 
 FLOPS = 2 * P * P * SEQS * PIECE
@@ -21,10 +23,10 @@ def tile_scatter_matmul_kernel(tc, base, x, w, b, offs, out):
         tc.tile_pool(name="held", bufs=1) as held,
         tc.psum_pool(name="windows", bufs=1) as windows,
     ):
-        base_tiles = [held.tile([P, TOKENS], BF16, name=f"base{i}") for i in range(SEQS)]
-        offsets = held.tile([P, SEQS * PIECE_COLS], U16, name="offsets")
-        x_tile = held.tile([P, SEQS * PIECE], BF16, name="x_tile")
-        w_tile = held.tile([P, P], BF16, name="w_tile")
+        base_tiles = [held.tile([P, TOKENS], BF16, name=f"base{i}", align_bytes=ROW_ALIGN) for i in range(SEQS)]
+        offsets = held.tile([P, SEQS * PIECE_COLS], U16, name="offsets", align_bytes=ROW_ALIGN)
+        x_tile = held.tile([P, SEQS * PIECE], BF16, name="x_tile", align_bytes=ROW_ALIGN)
+        w_tile = held.tile([P, P], BF16, name="w_tile", align_bytes=ROW_ALIGN)
         bias = held.tile([P, 1], F32, name="bias")
         nc.sync.dma_start(base_tiles[0][:], base[0])
         nc.sync.dma_start(base_tiles[1][:], base[1])
@@ -61,6 +63,6 @@ def tile_scatter_matmul_kernel(tc, base, x, w, b, offs, out):
             )
 
         for i in range(SEQS):
-            result = held.tile([P, TOKENS], F32, name=f"result{i}")
+            result = held.tile([P, TOKENS], F32, name=f"result{i}", align_bytes=ROW_ALIGN)
             nc.scalar.activation(result[:], window_tiles[i][:], GELU_TANH, bias=bias[:])
             nc.scalar.dma_start(out[i], result[:])

@@ -12,7 +12,7 @@ PIECE_COLS = PIECE // 16
 
 ROW_ALIGN = 256
 
-WARMING_MATMULS = 2
+WARMING_MATMULS = 3
 
 FLOPS = 2 * P * P * SEQS * PIECE
 
@@ -35,15 +35,21 @@ def tile_scatter_matmul_kernel(tc, base, x, w, b, offs, out):
         nc.scalar.dma_start(w_tile[:], w)
         nc.scalar.dma_start(bias[:], b)
 
-        zeros = held.tile([P, TOKENS], BF16, name="zeros")
+        zeros = held.tile([P, 1], BF16, name="zeros")
         nc.vector.memset(zeros[:], 0.0)
 
         table_warmer = held.tile([P, 1], F32, name="table_warmer")
-        nc.scalar.activation(table_warmer[:], zeros[:, 0:1], GELU_TANH)
+        nc.scalar.activation(table_warmer[:], zeros[:], GELU_TANH)
 
         idle_bank = windows.tile([P, TOKENS], F32, name="idle_bank")
         for warming in range(WARMING_MATMULS):
-            nc.tensor.matmul(idle_bank[:], zeros[:, 0:P], zeros[:], start=True, stop=True)
+            nc.tensor.matmul(
+                idle_bank[:],
+                zeros[:].to_broadcast([P, P]),
+                zeros[:].to_broadcast([P, TOKENS]),
+                start=True,
+                stop=True,
+            )
 
         identity = held.tile([P, P], BF16, name="identity")
         make_identity(nc, identity[:])

import concourse.mybir as mybir
from concourse.masks import make_identity

BF16, F32, U16 = mybir.dt.bfloat16, mybir.dt.float32, mybir.dt.uint16
GELU_TANH = mybir.ActivationFunctionType.Gelu_apprx_tanh

P = 128
SEQS = 2
TOKENS = 512
PIECE = 256
PIECE_COLS = PIECE // 16

ROW_ALIGN = 256

WARMING_MATMULS = 3

FLOPS = 2 * P * P * SEQS * PIECE


def tile_scatter_matmul_kernel(tc, base, x, w, b, offs, out):
    nc = tc.nc
    with (
        tc.tile_pool(name="held", bufs=1) as held,
        tc.psum_pool(name="windows", bufs=1) as windows,
    ):
        base_tiles = [held.tile([P, TOKENS], BF16, name=f"base{i}", align_bytes=ROW_ALIGN) for i in range(SEQS)]
        offsets = held.tile([P, SEQS * PIECE_COLS], U16, name="offsets", align_bytes=ROW_ALIGN)
        x_tile = held.tile([P, SEQS * PIECE], BF16, name="x_tile", align_bytes=ROW_ALIGN)
        w_tile = held.tile([P, P], BF16, name="w_tile", align_bytes=ROW_ALIGN)
        bias = held.tile([P, 1], F32, name="bias")
        nc.sync.dma_start(base_tiles[0][:], base[0])
        nc.sync.dma_start(base_tiles[1][:], base[1])
        nc.sync.dma_start(offsets[:], offs)
        nc.sync.dma_start(x_tile[:], x)
        nc.scalar.dma_start(w_tile[:], w)
        nc.scalar.dma_start(bias[:], b)

        zeros = held.tile([P, 1], BF16, name="zeros")
        nc.vector.memset(zeros[:], 0.0)

        table_warmer = held.tile([P, 1], F32, name="table_warmer")
        nc.scalar.activation(table_warmer[:], zeros[:], GELU_TANH)

        idle_bank = windows.tile([P, TOKENS], F32, name="idle_bank")
        for warming in range(WARMING_MATMULS):
            nc.tensor.matmul(
                idle_bank[:],
                zeros[:].to_broadcast([P, P]),
                zeros[:].to_broadcast([P, TOKENS]),
                start=True,
                stop=True,
            )

        identity = held.tile([P, P], BF16, name="identity")
        make_identity(nc, identity[:])

        window_tiles = [windows.tile([P, TOKENS], F32, name=f"window{i}") for i in range(SEQS)]
        for i in range(SEQS):
            nc.tensor.matmul(window_tiles[i][:], identity[:], base_tiles[i][:], start=True, stop=False)

        for i in range(SEQS):
            piece = offsets[:, i * PIECE_COLS : (i + 1) * PIECE_COLS]
            nc.tensor.matmul(
                window_tiles[i][:].indirect(piece),
                w_tile[:],
                x_tile[:, i * PIECE : (i + 1) * PIECE],
                start=False,
                stop=True,
            )

        for i in range(SEQS):
            result = held.tile([P, TOKENS], F32, name=f"result{i}", align_bytes=ROW_ALIGN)
            nc.scalar.activation(result[:], window_tiles[i][:], GELU_TANH, bias=bias[:])
            nc.scalar.dma_start(out[i], result[:])
